import numpy as np, ml_dtypes
CORES = [12,28,60,100,156,228]
N = 6
import mx_ref
NC, KT, G, WT = 384, 1, 2, 1
C = np.float32(0.031)
BF = ml_dtypes.bfloat16
def cut(t, i, w=512):
    return t[:, w * i:w * i + w]
def tile(rs):
    return np.stack(rs, axis=2).reshape(128, -1).astype(BF)
def layer(w, X):
    out = []
    for i in range(G):
        for t in range(len(X)):
            p = mx_ref.matmul(mx_ref.quantize(cut(w, len(X) * i + t)), X[t])
            z = p if t == 0 else z + p
        out.append(z)
    return out
def act(Z):
    return [np.maximum(s * z, 0) * C for z in Z for s in (1, -1)]
def setup_inputs(rng):
    def f(*shape):
        return mx_ref.flush((rng.standard_normal(shape, dtype=np.float32) * np.exp2(rng.integers(-2, 3, shape[:-1] + (1,)))).astype(BF))
    return {"x": f(N, 128, KT * 4 * NC), "w1": f(N, 128, G * KT * 512), "w2": f(N, 128, WT * 512)}
def setup_inputs_blocks(rng):
    d = setup_inputs(rng)
    for k in ("x", "w1", "w2"): d[k] = mx_ref.spread(d[k], rng, 4)
    return d
def setup_inputs_wide(rng):
    d = setup_inputs(rng)
    for k in ("x", "w1", "w2"): d[k] = mx_ref.flush((d[k].astype(np.float32) * np.exp2(rng.integers(-8, 9, (N, 1, 1))).astype(np.float32)).astype(BF))
    return d
def setup_inputs_zeros(rng):
    d = setup_inputs(rng); v = d["x"].reshape(N, 128, -1, 4).copy()
    v[np.broadcast_to((rng.random((N, 1, v.shape[2], 1)) < 0.33), v.shape)] = 0
    d["x"] = v.reshape(d["x"].shape)
    return d
def reference(x, w1, w2):
    H = [mx_ref.quantize(tile(act(layer(w1[j], [mx_ref.quantize(cut(x[j], t, 4 * NC)) for t in range(KT)])))) for j in range(N)]
    y = np.zeros((N, 128, N * WT * NC), np.float32)
    for r in range(N):
        for i in range(WT):
            qw = mx_ref.quantize(cut(w2[r], i))
            for j in range(N):
                y[r][:, NC * (WT * j + i):NC * (WT * j + i) + NC] = mx_ref.matmul(qw, H[j])
    return {"y": y}

@@ -1,0 +1,199 @@
+from concourse.bass import DstId, RemoteDMATransfer
+from concourse.mybir import dt, AluOpType, ActivationFunctionType
+
+N = 6
+W = 384
+HALF = W // 2
+SCALE = 0.031
+
+SCRATCH = {
+    "xb": ("sbuf", [128, 4 * W], "bfloat16"),
+    "w1b": ("sbuf", [128, 1024], "bfloat16"),
+    "w2b": ("sbuf", [128, 512], "bfloat16"),
+    "hb": ("sbuf", [128, 4 * W], "bfloat16"),
+    "xq": ("sbuf", [128, W], "float8_e4m3fn_x4"),
+    "xs": ("sbuf", [128, W], "uint8"),
+    "w1q": ("sbuf", [128, 256], "float8_e4m3fn_x4"),
+    "w1s": ("sbuf", [128, 256], "uint8"),
+    "w2q": ("sbuf", [128, 128], "float8_e4m3fn_x4"),
+    "w2s": ("sbuf", [128, 128], "uint8"),
+    "tq": ("sbuf", [128, N * W], "float8_e4m3fn_x4"),
+    "ts": ("sbuf", [128, N * W], "uint8"),
+    "yb": ("sbuf", [128, N * W], "float32"),
+    "ps": ("psum", [128, 512 * 8], "float32"),
+}
+SEMAPHORES = (["lx0", "lx1", "lw1", "lw2", "qw0", "qw1", "qx0", "qx1", "qw2", "hq0", "hq1", "sent", "stored"]
+              + ["z%d" % k for k in range(4)] + ["a%d" % k for k in range(8)]
+              + ["arr%d" % j for j in range(N)]
+              + ["m%d" % k for k in range(2 * N)] + ["c%d" % k for k in range(2 * N)])
+
+PLAN = {
+    ("main", 0): [(0, [("far0", 0)], [("main", 1)]), (0, [], [("near0", 4)])],
+    ("far0", 0): [(0, [], [("main", 3)]), (0, [], [("main", 2)])],
+    ("main", 1): [(1, [], [("far1", 4)]), (1, [("far0", 1)], [("main", 2)])],
+    ("far0", 1): [(1, [], [("main", 0)]), (1, [], [("main", 3)])],
+    ("main", 2): [(2, [], [("main", 0)]), (2, [("far1", 2)], [("far0", 4)]), (2, [], [("main", 1)])],
+    ("far1", 2): [(2, [], [("main", 3)])],
+    ("near0", 4): [(0, [("main", 4)], [("main", 5)])],
+    ("far1", 4): [(1, [("main", 4)], [("main", 5)])],
+    ("far0", 4): [(2, [("main", 4)], [("main", 5)])],
+    ("main", 3): [(3, [("far1", 3), ("far0", 3)], [("mfar1", 0)]), (3, [], [("main", 5)])],
+    ("mfar1", 0): [(3, [], [("main", 4)])],
+    ("far0", 3): [(3, [], [("main", 0)])],
+    ("far1", 3): [(3, [], [("main", 2)]), (3, [], [("main", 1)])],
+    ("main", 4): [(4, [("near1", 4)], [("main", 1)]), (4, [], [("sib", 2)])],
+    ("near1", 4): [(4, [], [("main", 3)]), (4, [], [("main", 5)])],
+    ("sib", 2): [(4, [("main", 2)], [("main", 0)])],
+    ("main", 5): [(5, [("far0", 5)], [("near1", 3)]), (5, [], [("mfar1", 2)])],
+    ("far0", 5): [(5, [], [("main", 4)])],
+    ("near1", 3): [(5, [("main", 3)], [("main", 0)]), (5, [], [("main", 1)])],
+    ("mfar1", 2): [(5, [], [("main", 2)])],
+}
+ORDER = [[0, 2, 1, 5, 3, 4], [1, 0, 4, 2, 5, 3], [2, 1, 3, 5, 4, 0], [3, 4, 5, 2, 0, 1], [4, 3, 1, 2, 0, 5], [5, 3, 1, 4, 2, 0]]
+
+
+def roles(T, topo):
+    cores = range(256)
+    R = {}
+    for i, m in enumerate(T.cores):
+        own = [c for c in cores if topo.host(c) == topo.host(m) and topo.chip(c) == topo.chip(m)]
+        mate = [c for c in cores if topo.mates(c, m)]
+        R["main", i] = m
+        for tag, here, there in (("", own, mate), ("m", mate, own)):
+            port = [c for c in here if c != m and topo.may_write(c, there[0])]
+            near = [c for c in port if topo.die(c) == topo.die(m)]
+            far = [c for c in port if topo.die(c) != topo.die(m)]
+            for k in range(2):
+                R["%snear%d" % (tag, k), i] = near[k]
+                R["%sfar%d" % (tag, k), i] = far[k]
+            if not tag:
+                R["sib", i] = [c for c in own if c != m and c not in port and topo.die(c) == topo.die(m)][0]
+    return R
+
+
+def masks(R, topo):
+    off = topo.mask(R["main", 0], R["main", 1])
+    on = topo.mask(R["main", 0], R["sib", 0])
+    return off, on & ~off
+
+
+def count(mask):
+    return bin(mask).count("1")
+
+
+def rank_program(g, core, T, topo):
+    R = roles(T, topo)
+    rank = T.rank_of(core)
+    name = [k for k in PLAN if R[k] == core]
+    if rank is not None:
+        compute(g, T, rank, R, topo)
+    for k in name:
+        forward(g, core, T, topo, R, PLAN[k], rank)
+
+
+def arrivals(R, topo):
+    off, on = masks(R, topo)
+    A = {}
+    for k in PLAN:
+        for tile, ons, offs in PLAN[k]:
+            for d in ons:
+                A[R[d], tile] = 2 * count(on)
+            for d in offs:
+                A[R[d], tile] = 2 * count(off)
+    return A
+
+
+def forward(g, core, T, topo, R, groups, rank):
+    off, on = masks(R, topo)
+    A = arrivals(R, topo)
+    seen = set()
+    sent = 0
+    for tile, ons, offs in groups:
+        if tile not in seen:
+            seen.add(tile)
+            if tile == rank:
+                g.wait_ge(T.sem["hq0"], 1)
+                g.wait_ge(T.sem["hq1"], 1)
+            else:
+                g.wait_ge(T.sem["arr%d" % tile], A[core, tile])
+        a, b = tile * W, tile * W + W
+        for plane in (False, True):
+            view = T.ts[:, a:b] if plane else T.tq[:, a:b].bitcast(dt.uint8)
+            trs = []
+            for ds, m in ((offs, off), (ons, on)):
+                if ds:
+                    ids = []
+                    for d in ds:
+                        rid, pid = topo.addr(R[d], core)
+                        ids.append(DstId(rid=rid, pnc=pid))
+                    trs.append(RemoteDMATransfer(dst_ids=ids, dma_engine_mask=m, remote_sem=T.sem["arr%d" % tile],
+                                                 srcs=[view], dsts=[view for _ in ds], alu_op=0))
+                    sent += count(m)
+            g.remote_dma_fused(trs, local_sem=T.sem.sent)
+    g.wait_ge(T.sem.sent, sent)
+
+
+def compute(g, T, rank, R, topo):
+    sem = T.sem
+    A = arrivals(R, topo)
+    main = R["main", rank]
+    t, v, s = g.tensor, g.vector, g.scalar
+    relu = ActivationFunctionType.Relu
+    X = 4 * HALF
+    g.sync.dma_start(T.xb[:, 0:X], T.x[:, 0:X]).then_inc(sem.lx0, 16)
+    s.dma_start(T.w1b[:], T.w1[:]).then_inc(sem.lw1, 16)
+    g.sync.dma_start(T.xb[:, X:2 * X], T.x[:, X:2 * X]).then_inc(sem.lx1, 16)
+    s.dma_start(T.w2b[:], T.w2[:]).then_inc(sem.lw2, 16)
+    v.wait_ge(sem.lw1, 16)
+    for i in range(2):
+        v.quantize_mx(T.w1q[:, 128 * i:128 * i + 128], T.w1s[:, 128 * i:128 * i + 128],
+                      T.w1b[:, 512 * i:512 * i + 512]).then_inc(sem["qw%d" % i], 1)
+    for k in range(2):
+        v.wait_ge(sem["lx%d" % k], 16)
+        v.quantize_mx(T.xq[:, HALF * k:HALF * k + HALF], T.xs[:, HALF * k:HALF * k + HALF],
+                      T.xb[:, X * k:X * k + X]).then_inc(sem["qx%d" % k], 1)
+    for k in range(2):
+        t.wait_ge(sem["qx%d" % k], 1)
+        for i in range(2):
+            if k == 0:
+                t.wait_ge(sem["qw%d" % i], 1)
+            q = 2 * k + i
+            t.matmul_mx(T.ps[:, 512 * q:512 * q + HALF], T.w1q[:, 128 * i:128 * i + 128], T.w1s[:, 128 * i:128 * i + 128],
+                        T.xq[:, HALF * k:HALF * k + HALF], T.xs[:, HALF * k:HALF * k + HALF], True, True).then_inc(sem["z%d" % q], 1)
+    for k in range(2):
+        s.wait_ge(sem["z%d" % (2 * k)], 1)
+        v.wait_ge(sem["z%d" % (2 * k + 1)], 1)
+        for b in range(2):
+            c = SCALE if b == 0 else -SCALE
+            s.activation(T.hb[:, X * k + b:X * k + X:4], T.ps[:, 1024 * k:1024 * k + HALF], relu,
+                         scale=c).then_inc(sem["a%d" % (4 * k + b)], 1)
+            v.tensor_scalar(T.hb[:, X * k + 2 + b:X * k + X:4], T.ps[:, 1024 * k + 512:1024 * k + 512 + HALF], c, 0.0,
+                            AluOpType.mult, AluOpType.max).then_inc(sem["a%d" % (4 * k + 2 + b)], 1)
+    for k in range(2):
+        for b in range(4):
+            v.wait_ge(sem["a%d" % (4 * k + b)], 1)
+        a = rank * W + HALF * k
+        v.quantize_mx(T.tq[:, a:a + HALF], T.ts[:, a:a + HALF], T.hb[:, X * k:X * k + X]).then_inc(sem["hq%d" % k], 1)
+    v.wait_ge(sem.lw2, 16)
+    v.quantize_mx(T.w2q[:], T.w2s[:], T.w2b[:]).then_inc(sem.qw2, 1)
+    t.wait_ge(sem.qw2, 1)
+    t.wait_ge(sem.hq0, 1)
+    t.wait_ge(sem.hq1, 1)
+    for n, j in enumerate(ORDER[rank]):
+        if j != rank:
+            t.wait_ge(sem["arr%d" % j], A[main, j])
+        for f, eng in ((0, s), (1, v)):
+            q = 2 * n + f
+            if q >= 8:
+                t.wait_ge(sem["c%d" % (q - 8)], 1)
+            a = j * W + HALF * f
+            P = T.ps[:, 512 * (q % 8):512 * (q % 8) + HALF]
+            t.matmul_mx(P, T.w2q[:], T.w2s[:], T.tq[:, a:a + HALF], T.ts[:, a:a + HALF], True, True).then_inc(sem["m%d" % q], 1)
+            eng.wait_ge(sem["m%d" % q], 1)
+            if f == 0:
+                s.activation(T.yb[:, a:a + HALF], P, ActivationFunctionType.Copy).then_inc(sem["c%d" % q], 1)
+            else:
+                v.tensor_copy(T.yb[:, a:a + HALF], P).then_inc(sem["c%d" % q], 1)
+            g.sync.wait_ge(sem["c%d" % q], 1)
+        g.sync.dma_start(T.y[:, j * W:j * W + W], T.yb[:, j * W:j * W + W]).then_inc(sem.stored, 16)
+    g.sync.wait_ge(sem.stored, 16 * N)

@@ -4,7 +4,11 @@ from concourse.mybir import dt, AluOpType, ActivationFunctionType
 N = 6
 W = 384
 HALF = W // 2
+K = 3
+P = W // K
 SCALE = 0.031
+
+SEQ = [("p", True, 0, W, True), ("c", False, 0, W, False)]
 
 SCRATCH = {
     "xb": ("sbuf", [128, 4 * W], "bfloat16"),
@@ -22,34 +26,39 @@ SCRATCH = {
     "yb": ("sbuf", [128, N * W], "float32"),
     "ps": ("psum", [128, 512 * 8], "float32"),
 }
-SEMAPHORES = (["lx0", "lx1", "lw1", "lw2", "qw0", "qw1", "qx0", "qx1", "qw2", "hq0", "hq1", "sent", "stored"]
-              + ["z%d" % k for k in range(4)] + ["a%d" % k for k in range(8)]
-              + ["arr%d" % j for j in range(N)]
-              + ["m%d" % k for k in range(2 * N)] + ["c%d" % k for k in range(2 * N)])
+SEMAPHORES = (["lw1", "lw2", "qw0", "qw1", "qw2", "sent", "stored"]
+              + ["%s%d" % (s, k) for s in ("lx", "qx", "hq") for k in range(K)]
+              + ["z%d" % k for k in range(2 * K)] + ["a%d" % k for k in range(4 * K)]
+              + ["%s%d" % (part[0], j) for part in SEQ for j in range(N)]
+              + ["m%d" % k for k in range(2 * N)] + ["d%d" % k for k in range(2 * N)])
 
 PLAN = {
-    ("main", 0): [(0, [("far0", 0)], [("main", 1)]), (0, [], [("near0", 4)])],
-    ("far0", 0): [(0, [], [("main", 3)]), (0, [], [("main", 2)])],
-    ("main", 1): [(1, [], [("far1", 4)]), (1, [("far0", 1)], [("main", 2)])],
-    ("far0", 1): [(1, [], [("main", 0)]), (1, [], [("main", 3)])],
-    ("main", 2): [(2, [], [("main", 0)]), (2, [("far1", 2)], [("far0", 4)]), (2, [], [("main", 1)])],
-    ("far1", 2): [(2, [], [("main", 3)])],
-    ("near0", 4): [(0, [("main", 4)], [("main", 5)])],
-    ("far1", 4): [(1, [("main", 4)], [("main", 5)])],
-    ("far0", 4): [(2, [("main", 4)], [("main", 5)])],
-    ("main", 3): [(3, [("far1", 3), ("far0", 3)], [("mfar1", 0)]), (3, [], [("main", 5)])],
-    ("mfar1", 0): [(3, [], [("main", 4)])],
-    ("far0", 3): [(3, [], [("main", 0)])],
-    ("far1", 3): [(3, [], [("main", 2)]), (3, [], [("main", 1)])],
-    ("main", 4): [(4, [("near1", 4)], [("main", 1)]), (4, [], [("sib", 2)])],
-    ("near1", 4): [(4, [], [("main", 3)]), (4, [], [("main", 5)])],
-    ("sib", 2): [(4, [("main", 2)], [("main", 0)])],
-    ("main", 5): [(5, [("far0", 5)], [("near1", 3)]), (5, [], [("mfar1", 2)])],
-    ("far0", 5): [(5, [], [("main", 4)])],
-    ("near1", 3): [(5, [("main", 3)], [("main", 0)]), (5, [], [("main", 1)])],
-    ("mfar1", 2): [(5, [], [("main", 2)])],
+    ("main", 0): [(0, [("near0", 4), ("near1", 0), ("main", 2)])],
+    ("near1", 0): [(0, [("main", 1), ("main", 3)])],
+    ("near0", 4): [(0, [("main", 4), ("main", 5)])],
+    ("main", 1): [(1, [("far1", 1), ("near0", 1), ("far0", 4)])],
+    ("far1", 1): [(1, [("main", 0), ("main", 2)])],
+    ("near0", 1): [(1, [("main", 3)])],
+    ("far0", 4): [(1, [("main", 5), ("main", 4)])],
+    ("main", 2): [(2, [("near1", 2), ("osib0", 2), ("far1", 0), ("mnear1", 3)])],
+    ("far1", 0): [(2, [("main", 0)])],
+    ("near1", 2): [(2, [("main", 5), ("main", 1)])],
+    ("mnear1", 3): [(2, [("main", 3)])],
+    ("osib0", 2): [(2, [("main", 4)])],
+    ("main", 3): [(3, [("near1", 5), ("near0", 3), ("mfar1", 1)])],
+    ("near0", 3): [(3, [("main", 2), ("main", 0)])],
+    ("mfar1", 1): [(3, [("main", 1)])],
+    ("near1", 5): [(3, [("main", 5), ("main", 4)])],
+    ("main", 4): [(4, [("far0", 2), ("far1", 4), ("mfar1", 5)])],
+    ("far0", 2): [(4, [("main", 3), ("main", 0), ("main", 2)])],
+    ("far1", 4): [(4, [("main", 1)])],
+    ("mfar1", 5): [(4, [("main", 5)])],
+    ("main", 5): [(5, [("far0", 3), ("far0", 5), ("mfar0", 0)])],
+    ("mfar0", 0): [(5, [("main", 0)])],
+    ("far0", 3): [(5, [("main", 3), ("main", 1)])],
+    ("far0", 5): [(5, [("main", 2), ("main", 4)])],
 }
-ORDER = [[0, 2, 1, 5, 3, 4], [1, 0, 4, 2, 5, 3], [2, 1, 3, 5, 4, 0], [3, 4, 5, 2, 0, 1], [4, 3, 1, 2, 0, 5], [5, 3, 1, 4, 2, 0]]
+ORDER = [[0, 2, 1, 3, 5, 4], [1, 4, 0, 5, 2, 3], [2, 5, 0, 3, 4, 1], [3, 5, 4, 1, 2, 0], [4, 1, 0, 3, 2, 5], [5, 3, 2, 1, 0, 4]]
 
 
 def roles(T, topo):
@@ -67,7 +76,10 @@ def roles(T, topo):
                 R["%snear%d" % (tag, k), i] = near[k]
                 R["%sfar%d" % (tag, k), i] = far[k]
             if not tag:
-                R["sib", i] = [c for c in own if c != m and c not in port and topo.die(c) == topo.die(m)][0]
+                rest = [c for c in own if c != m and c not in port]
+                R["sib", i] = [c for c in rest if topo.die(c) == topo.die(m)][0]
+                for k in range(2):
+                    R["osib%d" % k, i] = [c for c in rest if topo.die(c) != topo.die(m)][k]
     return R
 
 
@@ -81,55 +93,60 @@ def count(mask):
     return bin(mask).count("1")
 
 
+def samechip(topo, a, b):
+    return topo.host(a) == topo.host(b) and topo.chip(a) == topo.chip(b)
+
+
 def rank_program(g, core, T, topo):
     R = roles(T, topo)
     rank = T.rank_of(core)
-    name = [k for k in PLAN if R[k] == core]
     if rank is not None:
         compute(g, T, rank, R, topo)
-    for k in name:
-        forward(g, core, T, topo, R, PLAN[k], rank)
+    for k in PLAN:
+        if R[k] == core:
+            forward(g, core, T, topo, R, PLAN[k], rank)
 
 
 def arrivals(R, topo):
     off, on = masks(R, topo)
     A = {}
     for k in PLAN:
-        for tile, ons, offs in PLAN[k]:
-            for d in ons:
-                A[R[d], tile] = 2 * count(on)
-            for d in offs:
-                A[R[d], tile] = 2 * count(off)
+        for tile, kids in PLAN[k]:
+            for d in kids:
+                A[R[d], tile] = count(on if samechip(topo, R[k], R[d]) else off)
     return A
 
 
-def forward(g, core, T, topo, R, groups, rank):
+def forward(g, core, T, topo, R, sends, rank):
     off, on = masks(R, topo)
     A = arrivals(R, topo)
-    seen = set()
     sent = 0
-    for tile, ons, offs in groups:
-        if tile not in seen:
-            seen.add(tile)
+    for tile, kids in sends:
+        ons = [R[d] for d in kids if samechip(topo, R[d], core)]
+        offs = [R[d] for d in kids if not samechip(topo, R[d], core)]
+        groups = [(offs[i:i + 1], ons if i == 0 else []) for i in range(max(1, len(offs)))]
+        made = 0
+        for part, plane, lo, hi, together in SEQ:
             if tile == rank:
-                g.wait_ge(T.sem["hq0"], 1)
-                g.wait_ge(T.sem["hq1"], 1)
+                while P * made < hi:
+                    g.wait_ge(T.sem["hq%d" % made], 1)
+                    made += 1
             else:
-                g.wait_ge(T.sem["arr%d" % tile], A[core, tile])
-        a, b = tile * W, tile * W + W
-        for plane in (False, True):
+                g.wait_ge(T.sem["%s%d" % (part, tile)], A[core, tile])
+            a, b = tile * W + lo, tile * W + hi
             view = T.ts[:, a:b] if plane else T.tq[:, a:b].bitcast(dt.uint8)
-            trs = []
-            for ds, m in ((offs, off), (ons, on)):
-                if ds:
-                    ids = []
-                    for d in ds:
-                        rid, pid = topo.addr(R[d], core)
-                        ids.append(DstId(rid=rid, pnc=pid))
-                    trs.append(RemoteDMATransfer(dst_ids=ids, dma_engine_mask=m, remote_sem=T.sem["arr%d" % tile],
-                                                 srcs=[view], dsts=[view for _ in ds], alu_op=0))
-                    sent += count(m)
-            g.remote_dma_fused(trs, local_sem=T.sem.sent)
+            for outs, ins in ([(offs, ons)] if together else groups):
+                trs = []
+                for ds, m in ((outs, off), (ins, on)):
+                    if ds:
+                        ids = []
+                        for d in ds:
+                            rid, pid = topo.addr(d, core)
+                            ids.append(DstId(rid=rid, pnc=pid))
+                        trs.append(RemoteDMATransfer(dst_ids=ids, dma_engine_mask=m, remote_sem=T.sem["%s%d" % (part, tile)],
+                                                     srcs=[view], dsts=[view for _ in ds], alu_op=0))
+                        sent += count(m)
+                g.remote_dma_fused(trs, local_sem=T.sem.sent)
     g.wait_ge(T.sem.sent, sent)
 
 
@@ -139,61 +156,81 @@ def compute(g, T, rank, R, topo):
     main = R["main", rank]
     t, v, s = g.tensor, g.vector, g.scalar
     relu = ActivationFunctionType.Relu
-    X = 4 * HALF
-    g.sync.dma_start(T.xb[:, 0:X], T.x[:, 0:X]).then_inc(sem.lx0, 16)
+    X = 4 * P
     s.dma_start(T.w1b[:], T.w1[:]).then_inc(sem.lw1, 16)
-    g.sync.dma_start(T.xb[:, X:2 * X], T.x[:, X:2 * X]).then_inc(sem.lx1, 16)
-    s.dma_start(T.w2b[:], T.w2[:]).then_inc(sem.lw2, 16)
+    for k in range(K):
+        g.sync.dma_start(T.xb[:, X * k:X * k + X], T.x[:, X * k:X * k + X]).then_inc(sem["lx%d" % k], 16)
+    g.sync.wait_ge(sem.lx0, 16)
+    g.sync.dma_start(T.w2b[:], T.w2[:]).then_inc(sem.lw2, 16)
     v.wait_ge(sem.lw1, 16)
     for i in range(2):
         v.quantize_mx(T.w1q[:, 128 * i:128 * i + 128], T.w1s[:, 128 * i:128 * i + 128],
                       T.w1b[:, 512 * i:512 * i + 512]).then_inc(sem["qw%d" % i], 1)
-    for k in range(2):
+    for k in range(K):
         v.wait_ge(sem["lx%d" % k], 16)
-        v.quantize_mx(T.xq[:, HALF * k:HALF * k + HALF], T.xs[:, HALF * k:HALF * k + HALF],
+        v.quantize_mx(T.xq[:, P * k:P * k + P], T.xs[:, P * k:P * k + P],
                       T.xb[:, X * k:X * k + X]).then_inc(sem["qx%d" % k], 1)
-    for k in range(2):
+    for k in range(K):
         t.wait_ge(sem["qx%d" % k], 1)
         for i in range(2):
             if k == 0:
                 t.wait_ge(sem["qw%d" % i], 1)
             q = 2 * k + i
-            t.matmul_mx(T.ps[:, 512 * q:512 * q + HALF], T.w1q[:, 128 * i:128 * i + 128], T.w1s[:, 128 * i:128 * i + 128],
-                        T.xq[:, HALF * k:HALF * k + HALF], T.xs[:, HALF * k:HALF * k + HALF], True, True).then_inc(sem["z%d" % q], 1)
-    for k in range(2):
-        s.wait_ge(sem["z%d" % (2 * k)], 1)
-        v.wait_ge(sem["z%d" % (2 * k + 1)], 1)
+            t.matmul_mx(T.ps[:, 512 * q:512 * q + P], T.w1q[:, 128 * i:128 * i + 128], T.w1s[:, 128 * i:128 * i + 128],
+                        T.xq[:, P * k:P * k + P], T.xs[:, P * k:P * k + P], True, True).then_inc(sem["z%d" % q], 1)
+
+    def steps(k, i, eng):
+        q = 2 * k + i
+        eng.wait_ge(sem["z%d" % q], 1)
         for b in range(2):
             c = SCALE if b == 0 else -SCALE
-            s.activation(T.hb[:, X * k + b:X * k + X:4], T.ps[:, 1024 * k:1024 * k + HALF], relu,
-                         scale=c).then_inc(sem["a%d" % (4 * k + b)], 1)
-            v.tensor_scalar(T.hb[:, X * k + 2 + b:X * k + X:4], T.ps[:, 1024 * k + 512:1024 * k + 512 + HALF], c, 0.0,
-                            AluOpType.mult, AluOpType.max).then_inc(sem["a%d" % (4 * k + 2 + b)], 1)
-    for k in range(2):
+            out = T.hb[:, X * k + 2 * i + b:X * k + X:4]
+            z = T.ps[:, 512 * q:512 * q + P]
+            done = sem["a%d" % (4 * k + 2 * i + b)]
+            if eng is s:
+                s.activation(out, z, relu, scale=c).then_inc(done, 1)
+            else:
+                v.tensor_scalar(out, z, c, 0.0, AluOpType.mult, AluOpType.max).then_inc(done, 1)
+
+    def pack(k):
         for b in range(4):
             v.wait_ge(sem["a%d" % (4 * k + b)], 1)
-        a = rank * W + HALF * k
-        v.quantize_mx(T.tq[:, a:a + HALF], T.ts[:, a:a + HALF], T.hb[:, X * k:X * k + X]).then_inc(sem["hq%d" % k], 1)
+        a = rank * W + P * k
+        v.quantize_mx(T.tq[:, a:a + P], T.ts[:, a:a + P], T.hb[:, X * k:X * k + X]).then_inc(sem["hq%d" % k], 1)
+
+    steps(0, 0, s)
+    steps(0, 1, s)
+    steps(1, 1, s)
+    steps(2, 1, s)
+    steps(1, 0, v)
+    pack(0)
+    steps(2, 0, v)
+    pack(1)
+    pack(2)
     v.wait_ge(sem.lw2, 16)
     v.quantize_mx(T.w2q[:], T.w2s[:], T.w2b[:]).then_inc(sem.qw2, 1)
     t.wait_ge(sem.qw2, 1)
-    t.wait_ge(sem.hq0, 1)
-    t.wait_ge(sem.hq1, 1)
+    for k in range(K):
+        t.wait_ge(sem["hq%d" % k], 1)
     for n, j in enumerate(ORDER[rank]):
         if j != rank:
-            t.wait_ge(sem["arr%d" % j], A[main, j])
+            for part in SEQ:
+                t.wait_ge(sem["%s%d" % (part[0], j)], A[main, j])
         for f, eng in ((0, s), (1, v)):
             q = 2 * n + f
             if q >= 8:
-                t.wait_ge(sem["c%d" % (q - 8)], 1)
+                t.wait_ge(sem["d%d" % (q - 8)], 1)
             a = j * W + HALF * f
-            P = T.ps[:, 512 * (q % 8):512 * (q % 8) + HALF]
-            t.matmul_mx(P, T.w2q[:], T.w2s[:], T.tq[:, a:a + HALF], T.ts[:, a:a + HALF], True, True).then_inc(sem["m%d" % q], 1)
+            z = T.ps[:, 512 * (q % 8):512 * (q % 8) + HALF]
+            t.matmul_mx(z, T.w2q[:], T.w2s[:], T.tq[:, a:a + HALF], T.ts[:, a:a + HALF], True, True).then_inc(sem["m%d" % q], 1)
             eng.wait_ge(sem["m%d" % q], 1)
             if f == 0:
-                s.activation(T.yb[:, a:a + HALF], P, ActivationFunctionType.Copy).then_inc(sem["c%d" % q], 1)
+                s.activation(T.yb[:, a:a + HALF], z, ActivationFunctionType.Copy).then_inc(sem["d%d" % q], 1)
             else:
-                v.tensor_copy(T.yb[:, a:a + HALF], P).then_inc(sem["c%d" % q], 1)
-            g.sync.wait_ge(sem["c%d" % q], 1)
+                v.tensor_copy(T.yb[:, a:a + HALF], z).then_inc(sem["d%d" % q], 1)
+    for n in [1, 0] + list(range(2, N)):
+        j = ORDER[rank][n]
+        for f in range(2):
+            g.sync.wait_ge(sem["d%d" % (2 * n + f)], 1)
         g.sync.dma_start(T.y[:, j * W:j * W + W], T.yb[:, j * W:j * W + W]).then_inc(sem.stored, 16)
     g.sync.wait_ge(sem.stored, 16 * N)

from concourse.bass import DstId, RemoteDMATransfer
from concourse.mybir import dt, AluOpType, ActivationFunctionType

N = 6
W = 384
HALF = W // 2
K = 3
P = W // K
SCALE = 0.031

SEQ = [("p", True, 0, W, True), ("c", False, 0, W, False)]

SCRATCH = {
    "xb": ("sbuf", [128, 4 * W], "bfloat16"),
    "w1b": ("sbuf", [128, 1024], "bfloat16"),
    "w2b": ("sbuf", [128, 512], "bfloat16"),
    "hb": ("sbuf", [128, 4 * W], "bfloat16"),
    "xq": ("sbuf", [128, W], "float8_e4m3fn_x4"),
    "xs": ("sbuf", [128, W], "uint8"),
    "w1q": ("sbuf", [128, 256], "float8_e4m3fn_x4"),
    "w1s": ("sbuf", [128, 256], "uint8"),
    "w2q": ("sbuf", [128, 128], "float8_e4m3fn_x4"),
    "w2s": ("sbuf", [128, 128], "uint8"),
    "tq": ("sbuf", [128, N * W], "float8_e4m3fn_x4"),
    "ts": ("sbuf", [128, N * W], "uint8"),
    "yb": ("sbuf", [128, N * W], "float32"),
    "ps": ("psum", [128, 512 * 8], "float32"),
}
SEMAPHORES = (["lw1", "lw2", "qw0", "qw1", "qw2", "sent", "stored"]
              + ["%s%d" % (s, k) for s in ("lx", "qx", "hq") for k in range(K)]
              + ["z%d" % k for k in range(2 * K)] + ["a%d" % k for k in range(4 * K)]
              + ["%s%d" % (part[0], j) for part in SEQ for j in range(N)]
              + ["m%d" % k for k in range(2 * N)] + ["d%d" % k for k in range(2 * N)])

PLAN = {
    ("main", 0): [(0, [("near0", 4), ("near1", 0), ("main", 2)])],
    ("near1", 0): [(0, [("main", 1), ("main", 3)])],
    ("near0", 4): [(0, [("main", 4), ("main", 5)])],
    ("main", 1): [(1, [("far1", 1), ("near0", 1), ("far0", 4)])],
    ("far1", 1): [(1, [("main", 0), ("main", 2)])],
    ("near0", 1): [(1, [("main", 3)])],
    ("far0", 4): [(1, [("main", 5), ("main", 4)])],
    ("main", 2): [(2, [("near1", 2), ("osib0", 2), ("far1", 0), ("mnear1", 3)])],
    ("far1", 0): [(2, [("main", 0)])],
    ("near1", 2): [(2, [("main", 5), ("main", 1)])],
    ("mnear1", 3): [(2, [("main", 3)])],
    ("osib0", 2): [(2, [("main", 4)])],
    ("main", 3): [(3, [("near1", 5), ("near0", 3), ("mfar1", 1)])],
    ("near0", 3): [(3, [("main", 2), ("main", 0)])],
    ("mfar1", 1): [(3, [("main", 1)])],
    ("near1", 5): [(3, [("main", 5), ("main", 4)])],
    ("main", 4): [(4, [("far0", 2), ("far1", 4), ("mfar1", 5)])],
    ("far0", 2): [(4, [("main", 3), ("main", 0), ("main", 2)])],
    ("far1", 4): [(4, [("main", 1)])],
    ("mfar1", 5): [(4, [("main", 5)])],
    ("main", 5): [(5, [("far0", 3), ("far0", 5), ("mfar0", 0)])],
    ("mfar0", 0): [(5, [("main", 0)])],
    ("far0", 3): [(5, [("main", 3), ("main", 1)])],
    ("far0", 5): [(5, [("main", 2), ("main", 4)])],
}
ORDER = [[0, 2, 1, 3, 5, 4], [1, 4, 0, 5, 2, 3], [2, 5, 0, 3, 4, 1], [3, 5, 4, 1, 2, 0], [4, 1, 0, 3, 2, 5], [5, 3, 2, 1, 0, 4]]


def roles(T, topo):
    cores = range(256)
    R = {}
    for i, m in enumerate(T.cores):
        own = [c for c in cores if topo.host(c) == topo.host(m) and topo.chip(c) == topo.chip(m)]
        mate = [c for c in cores if topo.mates(c, m)]
        R["main", i] = m
        for tag, here, there in (("", own, mate), ("m", mate, own)):
            port = [c for c in here if c != m and topo.may_write(c, there[0])]
            near = [c for c in port if topo.die(c) == topo.die(m)]
            far = [c for c in port if topo.die(c) != topo.die(m)]
            for k in range(2):
                R["%snear%d" % (tag, k), i] = near[k]
                R["%sfar%d" % (tag, k), i] = far[k]
            if not tag:
                rest = [c for c in own if c != m and c not in port]
                R["sib", i] = [c for c in rest if topo.die(c) == topo.die(m)][0]
                for k in range(2):
                    R["osib%d" % k, i] = [c for c in rest if topo.die(c) != topo.die(m)][k]
    return R


def masks(R, topo):
    off = topo.mask(R["main", 0], R["main", 1])
    on = topo.mask(R["main", 0], R["sib", 0])
    return off, on & ~off


def count(mask):
    return bin(mask).count("1")


def samechip(topo, a, b):
    return topo.host(a) == topo.host(b) and topo.chip(a) == topo.chip(b)


def rank_program(g, core, T, topo):
    R = roles(T, topo)
    rank = T.rank_of(core)
    if rank is not None:
        compute(g, T, rank, R, topo)
    for k in PLAN:
        if R[k] == core:
            forward(g, core, T, topo, R, PLAN[k], rank)


def arrivals(R, topo):
    off, on = masks(R, topo)
    A = {}
    for k in PLAN:
        for tile, kids in PLAN[k]:
            for d in kids:
                A[R[d], tile] = count(on if samechip(topo, R[k], R[d]) else off)
    return A


def forward(g, core, T, topo, R, sends, rank):
    off, on = masks(R, topo)
    A = arrivals(R, topo)
    sent = 0
    for tile, kids in sends:
        ons = [R[d] for d in kids if samechip(topo, R[d], core)]
        offs = [R[d] for d in kids if not samechip(topo, R[d], core)]
        groups = [(offs[i:i + 1], ons if i == 0 else []) for i in range(max(1, len(offs)))]
        made = 0
        for part, plane, lo, hi, together in SEQ:
            if tile == rank:
                while P * made < hi:
                    g.wait_ge(T.sem["hq%d" % made], 1)
                    made += 1
            else:
                g.wait_ge(T.sem["%s%d" % (part, tile)], A[core, tile])
            a, b = tile * W + lo, tile * W + hi
            view = T.ts[:, a:b] if plane else T.tq[:, a:b].bitcast(dt.uint8)
            for outs, ins in ([(offs, ons)] if together else groups):
                trs = []
                for ds, m in ((outs, off), (ins, on)):
                    if ds:
                        ids = []
                        for d in ds:
                            rid, pid = topo.addr(d, core)
                            ids.append(DstId(rid=rid, pnc=pid))
                        trs.append(RemoteDMATransfer(dst_ids=ids, dma_engine_mask=m, remote_sem=T.sem["%s%d" % (part, tile)],
                                                     srcs=[view], dsts=[view for _ in ds], alu_op=0))
                        sent += count(m)
                g.remote_dma_fused(trs, local_sem=T.sem.sent)
    g.wait_ge(T.sem.sent, sent)


def compute(g, T, rank, R, topo):
    sem = T.sem
    A = arrivals(R, topo)
    main = R["main", rank]
    t, v, s = g.tensor, g.vector, g.scalar
    relu = ActivationFunctionType.Relu
    X = 4 * P
    s.dma_start(T.w1b[:], T.w1[:]).then_inc(sem.lw1, 16)
    for k in range(K):
        g.sync.dma_start(T.xb[:, X * k:X * k + X], T.x[:, X * k:X * k + X]).then_inc(sem["lx%d" % k], 16)
    g.sync.wait_ge(sem.lx0, 16)
    g.sync.dma_start(T.w2b[:], T.w2[:]).then_inc(sem.lw2, 16)
    v.wait_ge(sem.lw1, 16)
    for i in range(2):
        v.quantize_mx(T.w1q[:, 128 * i:128 * i + 128], T.w1s[:, 128 * i:128 * i + 128],
                      T.w1b[:, 512 * i:512 * i + 512]).then_inc(sem["qw%d" % i], 1)
    for k in range(K):
        v.wait_ge(sem["lx%d" % k], 16)
        v.quantize_mx(T.xq[:, P * k:P * k + P], T.xs[:, P * k:P * k + P],
                      T.xb[:, X * k:X * k + X]).then_inc(sem["qx%d" % k], 1)
    for k in range(K):
        t.wait_ge(sem["qx%d" % k], 1)
        for i in range(2):
            if k == 0:
                t.wait_ge(sem["qw%d" % i], 1)
            q = 2 * k + i
            t.matmul_mx(T.ps[:, 512 * q:512 * q + P], T.w1q[:, 128 * i:128 * i + 128], T.w1s[:, 128 * i:128 * i + 128],
                        T.xq[:, P * k:P * k + P], T.xs[:, P * k:P * k + P], True, True).then_inc(sem["z%d" % q], 1)

    def steps(k, i, eng):
        q = 2 * k + i
        eng.wait_ge(sem["z%d" % q], 1)
        for b in range(2):
            c = SCALE if b == 0 else -SCALE
            out = T.hb[:, X * k + 2 * i + b:X * k + X:4]
            z = T.ps[:, 512 * q:512 * q + P]
            done = sem["a%d" % (4 * k + 2 * i + b)]
            if eng is s:
                s.activation(out, z, relu, scale=c).then_inc(done, 1)
            else:
                v.tensor_scalar(out, z, c, 0.0, AluOpType.mult, AluOpType.max).then_inc(done, 1)

    def pack(k):
        for b in range(4):
            v.wait_ge(sem["a%d" % (4 * k + b)], 1)
        a = rank * W + P * k
        v.quantize_mx(T.tq[:, a:a + P], T.ts[:, a:a + P], T.hb[:, X * k:X * k + X]).then_inc(sem["hq%d" % k], 1)

    steps(0, 0, s)
    steps(0, 1, s)
    steps(1, 1, s)
    steps(2, 1, s)
    steps(1, 0, v)
    pack(0)
    steps(2, 0, v)
    pack(1)
    pack(2)
    v.wait_ge(sem.lw2, 16)
    v.quantize_mx(T.w2q[:], T.w2s[:], T.w2b[:]).then_inc(sem.qw2, 1)
    t.wait_ge(sem.qw2, 1)
    for k in range(K):
        t.wait_ge(sem["hq%d" % k], 1)
    for n, j in enumerate(ORDER[rank]):
        if j != rank:
            for part in SEQ:
                t.wait_ge(sem["%s%d" % (part[0], j)], A[main, j])
        for f, eng in ((0, s), (1, v)):
            q = 2 * n + f
            if q >= 8:
                t.wait_ge(sem["d%d" % (q - 8)], 1)
            a = j * W + HALF * f
            z = T.ps[:, 512 * (q % 8):512 * (q % 8) + HALF]
            t.matmul_mx(z, T.w2q[:], T.w2s[:], T.tq[:, a:a + HALF], T.ts[:, a:a + HALF], True, True).then_inc(sem["m%d" % q], 1)
            eng.wait_ge(sem["m%d" % q], 1)
            if f == 0:
                s.activation(T.yb[:, a:a + HALF], z, ActivationFunctionType.Copy).then_inc(sem["d%d" % q], 1)
            else:
                v.tensor_copy(T.yb[:, a:a + HALF], z).then_inc(sem["d%d" % q], 1)
    for n in [1, 0] + list(range(2, N)):
        j = ORDER[rank][n]
        for f in range(2):
            g.sync.wait_ge(sem["d%d" % (2 * n + f)], 1)
        g.sync.dma_start(T.y[:, j * W:j * W + W], T.yb[:, j * W:j * W + W]).then_inc(sem.stored, 16)
    g.sync.wait_ge(sem.stored, 16 * N)
